import numpy as np
import ml_dtypes


def mxq(x, axis, fmt="e4m3"):
    dtype, down = {"e4m3": (ml_dtypes.float8_e4m3fn, 7), "e5m2": (ml_dtypes.float8_e5m2, 14)}[fmt]
    v = np.moveaxis(np.asarray(x, np.float32).astype(ml_dtypes.bfloat16).astype(np.float64), axis, -1)
    blocks = v.reshape(v.shape[:-1] + (-1, 32))
    amax = np.abs(blocks).max(-1, keepdims=True)
    byte = np.maximum(np.where(amax > 0, np.frexp(amax)[1] - 1 + 127, 0) - down, 1)
    scale = np.exp2(byte - 127.0)
    codes = (blocks / scale).astype(np.float32).astype(dtype).astype(np.float64)
    return np.moveaxis((codes * scale).reshape(v.shape), -1, axis)


WIDE = False


def mx_kscale(k):
    if not WIDE:
        return np.ones(k)
    levels = np.array([10, -10, 5, -5, 0])
    if k % 512:
        return np.exp2(np.random.permutation(np.resize(levels, k // 32))).repeat(32)
    a = np.empty((k // 512, 16))
    for p in range(k // 512):
        a[p, :8] = np.random.permutation(np.resize(levels, 8))
        for g in range(8):
            far = levels[np.abs(levels - a[p, g]) >= 10]
            a[p, g + 8] = far[np.random.randint(len(far))]
    return np.exp2(a.ravel()).repeat(32)


def f64(x):
    return np.asarray(x).astype(np.float64)


def striped(idx):
    return np.tile(np.asarray(idx).reshape(-1, 16).T, (8, 1)).astype(np.uint16)


def unstriped(offs):
    return offs[:16].T.reshape(-1).astype(np.int64)


G, K, T, D, M = 512, 2, 4096, 512, 512


def setup_inputs():
    n = np.random.standard_normal
    s = mx_kscale(D)[:, None]
    grid = lambda x: np.round(x * 32) / 32
    x = grid(n((D, T))) * s
    idx = np.random.randint(0, T, (G, K))
    return {
        "xT": x.astype(np.float32),
        "w": (n((D, M)) / np.sqrt(D * K) / s).astype(np.float32),
        "bias": (0.3 * n((M, 1))).astype(np.float32),
        "offs": striped(idx.reshape(-1)),
    }


def reference(xT, w, bias, offs):
    x = f64(xT)[:, unstriped(offs)]
    y = mxq(f64(w), 0, "e4m3").T @ mxq(x.reshape(D, G, K).sum(-1), 0, "e4m3")
    y = y + f64(bias)
    return y

@@ -1,0 +1,131 @@
+from contextlib import ExitStack
+
+import concourse.mybir as mybir
+from concourse.masks import make_identity
+
+D, T, G, BAG, M = 512, 4096, 512, 2, 512
+FLOPS = 2 * D * M * G
+
+F32 = mybir.dt.float32
+BF16 = mybir.dt.bfloat16
+U32 = mybir.dt.uint32
+U16 = mybir.dt.uint16
+U8 = mybir.dt.uint8
+FP8X4 = mybir.dt.float8_e4m3fn_x4
+ADD = mybir.AluOpType.add
+COPY = mybir.ActivationFunctionType.Copy
+IDENTITY = mybir.ActivationFunctionType.Identity
+
+P = 128
+PACK = 4
+HALVES = 2
+G_HALF = G // HALVES
+E_HALF = G_HALF * BAG
+LIST_HALF = E_HALF // 16
+M_HALF = M // HALVES
+M_TILES = M // P
+
+
+def tile_attend_bag_bias_kernel(tc, xT, w, bias, offs, out):
+    nc = tc.nc
+    with ExitStack() as ctx:
+        keep = ctx.enter_context(tc.tile_pool(name="keep", bufs=1))
+        psum = ctx.enter_context(tc.psum_pool(name="psum", bufs=8))
+
+        offsets = keep.tile([P, G * BAG // 16], U16, name="offsets")
+        nc.sync.dma_start(offsets[:], offs)
+
+        x_rows = xT.rearrange("(p t) c -> p t c", t=PACK)
+        planes = []
+        for t in range(PACK):
+            plane = keep.tile([P, T], F32, name="plane%d" % t)
+            nc.sync.dma_start(plane[:], x_rows[:, t, :])
+            planes.append(plane)
+        w_rows = w.rearrange("(p t) m -> p t m", t=PACK)
+        w_raw = []
+        for h in range(HALVES):
+            raw = keep.tile([P, PACK, M_HALF], F32, name="w_raw%d" % h)
+            nc.sync.dma_start(raw[:], w_rows[:, :, h * M_HALF : (h + 1) * M_HALF])
+            w_raw.append(raw)
+
+        ident = keep.tile([P, P], F32, name="ident")
+        make_identity(nc, ident[:])
+        bias_rows = keep.tile([P, P], F32, name="bias_rows")
+        nc.vector.memset(bias_rows[:], 0.0)
+        nc.scalar.dma_start(bias_rows[0:M_TILES, :], bias.rearrange("(t p) o -> t (p o)", p=P))
+        turned = psum.tile([P, 512], F32, name="acc")
+        nc.tensor.transpose(turned[:, 0:P], bias_rows[:], ident[:])
+        bias_cols = keep.tile([P, M_TILES], F32, name="bias_cols")
+        nc.scalar.copy(bias_cols[:], turned[:, 0:M_TILES])
+
+        picked = [keep.tile([P, PACK, E_HALF], F32, name="picked%d" % h) for h in range(HALVES)]
+        e_grouped = [keep.tile([P, G_HALF, PACK], BF16, name="e_grouped%d" % h, align_bytes=64) for h in range(HALVES)]
+        e_codes = [keep.tile([P, G_HALF], U32, name="e_codes%d" % h, align_bytes=64) for h in range(HALVES)]
+        e_scales = [keep.tile([P, G_HALF], U8, name="e_scales%d" % h, align_bytes=64) for h in range(HALVES)]
+        w_grouped = [keep.tile([P, M_HALF, PACK], BF16, name="w_grouped%d" % h, align_bytes=64) for h in range(HALVES)]
+        w_codes = [keep.tile([P, M_HALF], U32, name="w_codes%d" % h, align_bytes=64) for h in range(HALVES)]
+        w_scales = [keep.tile([P, M_HALF], U8, name="w_scales%d" % h, align_bytes=64) for h in range(HALVES)]
+        adder = [nc.gpsimd, nc.vector]
+
+        def gather(t, h):
+            nc.vector.tensor_copy(
+                picked[h][:, t, :],
+                planes[t][:].indirect(offsets[:, h * LIST_HALF : (h + 1) * LIST_HALF]),
+            )
+
+        def add(t0, t1, h):
+            entries = picked[h][:].rearrange("p t (g j) -> p j g t", j=BAG)
+            adder[h].tensor_tensor(
+                out=e_grouped[h][:, :, t0:t1], in0=entries[:, 0, :, t0:t1], in1=entries[:, 1, :, t0:t1], op=ADD
+            )
+
+        def quantize(grouped, codes, scales):
+            nc.vector.quantize_mx(
+                out=codes[:].bitcast(FP8X4), scales=scales[:], in_=grouped[:].rearrange("p c t -> p (c t)")
+            )
+
+        for t in range(PACK):
+            for h in range(HALVES):
+                gather(t, h)
+            if t > 0:
+                for h in range(HALVES):
+                    add(0 if t == 1 else t, t + 1, h)
+
+        for h in range(HALVES):
+            for u in range(M_HALF // P):
+                cols = slice(u * P, (u + 1) * P)
+                nc.scalar.activation(
+                    w_grouped[h][:, cols, :].rearrange("p (c i) t -> p c t i", i=4),
+                    w_raw[h][:, :, cols].rearrange("p t (c i) -> p c t i", i=4),
+                    COPY,
+                )
+        quantize(w_grouped[0], w_codes[0], w_scales[0])
+        for h in range(HALVES):
+            quantize(e_grouped[h], e_codes[h], e_scales[h])
+        quantize(w_grouped[1], w_codes[1], w_scales[1])
+
+        results = [keep.tile([P, G], F32, name="result%d" % m) for m in range(M_TILES)]
+        for wh in range(HALVES):
+            for h in range(HALVES):
+                for u in range(M_HALF // P):
+                    m = wh * (M_HALF // P) + u
+                    cols = slice(u * P, (u + 1) * P)
+                    acc = psum.tile([P, 512], F32, name="acc")
+                    nc.tensor.matmul_mx(
+                        out=acc[:, 0:G_HALF],
+                        lhsT=w_codes[wh][:, cols].bitcast(FP8X4),
+                        lhsT_scale=w_scales[wh][:, cols],
+                        rhs=e_codes[h][:].bitcast(FP8X4),
+                        rhs_scale=e_scales[h][:],
+                        start=True,
+                        stop=True,
+                    )
+                    dst = results[m][:, h * G_HALF : (h + 1) * G_HALF]
+                    if u == 0:
+                        nc.scalar.activation(dst, acc[:, 0:G_HALF], IDENTITY, bias=bias_cols[:, m : m + 1])
+                    else:
+                        nc.vector.tensor_scalar(dst, acc[:, 0:G_HALF], bias_cols[:, m : m + 1], None, ADD)
+            for u in range(M_HALF // P):
+                m = wh * (M_HALF // P) + u
+                queue = nc.scalar if u == 0 else nc.sync
+                queue.dma_start(out[m * P : (m + 1) * P, :], results[m][:])

@@ -1,7 +1,6 @@
 from contextlib import ExitStack
 
 import concourse.mybir as mybir
-from concourse.masks import make_identity
 
 D, T, G, BAG, M = 512, 4096, 512, 2, 512
 FLOPS = 2 * D * M * G
@@ -13,7 +12,6 @@ U16 = mybir.dt.uint16
 U8 = mybir.dt.uint8
 FP8X4 = mybir.dt.float8_e4m3fn_x4
 ADD = mybir.AluOpType.add
-COPY = mybir.ActivationFunctionType.Copy
 IDENTITY = mybir.ActivationFunctionType.Identity
 
 P = 128
@@ -23,7 +21,8 @@ G_HALF = G // HALVES
 E_HALF = G_HALF * BAG
 LIST_HALF = E_HALF // 16
 M_HALF = M // HALVES
-M_TILES = M // P
+TILES = M_HALF // P
+WIDTH = M_HALF + G_HALF
 
 
 def tile_attend_bag_bias_kernel(tc, xT, w, bias, offs, out):
@@ -47,24 +46,18 @@ def tile_attend_bag_bias_kernel(tc, xT, w, bias, offs, out):
             raw = keep.tile([P, PACK, M_HALF], F32, name="w_raw%d" % h)
             nc.sync.dma_start(raw[:], w_rows[:, :, h * M_HALF : (h + 1) * M_HALF])
             w_raw.append(raw)
+        bias_cols = keep.tile([P, HALVES, TILES], F32, name="bias_cols")
+        nc.sync.dma_start(bias_cols[:], bias.rearrange("(h p u) o -> p h (u o)", h=HALVES, u=TILES))
 
-        ident = keep.tile([P, P], F32, name="ident")
-        make_identity(nc, ident[:])
-        bias_rows = keep.tile([P, P], F32, name="bias_rows")
-        nc.vector.memset(bias_rows[:], 0.0)
-        nc.scalar.dma_start(bias_rows[0:M_TILES, :], bias.rearrange("(t p) o -> t (p o)", p=P))
-        turned = psum.tile([P, 512], F32, name="acc")
-        nc.tensor.transpose(turned[:, 0:P], bias_rows[:], ident[:])
-        bias_cols = keep.tile([P, M_TILES], F32, name="bias_cols")
-        nc.scalar.copy(bias_cols[:], turned[:, 0:M_TILES])
+        zero = keep.tile([P, 1], F32, name="zero")
+        nc.vector.memset(zero[:], 0.0)
+        loaded = keep.tile([P, 1], F32, name="loaded")
+        nc.scalar.activation(loaded[:], zero[:], IDENTITY)
 
         picked = [keep.tile([P, PACK, E_HALF], F32, name="picked%d" % h) for h in range(HALVES)]
-        e_grouped = [keep.tile([P, G_HALF, PACK], BF16, name="e_grouped%d" % h, align_bytes=64) for h in range(HALVES)]
-        e_codes = [keep.tile([P, G_HALF], U32, name="e_codes%d" % h, align_bytes=64) for h in range(HALVES)]
-        e_scales = [keep.tile([P, G_HALF], U8, name="e_scales%d" % h, align_bytes=64) for h in range(HALVES)]
-        w_grouped = [keep.tile([P, M_HALF, PACK], BF16, name="w_grouped%d" % h, align_bytes=64) for h in range(HALVES)]
-        w_codes = [keep.tile([P, M_HALF], U32, name="w_codes%d" % h, align_bytes=64) for h in range(HALVES)]
-        w_scales = [keep.tile([P, M_HALF], U8, name="w_scales%d" % h, align_bytes=64) for h in range(HALVES)]
+        grouped = [keep.tile([P, WIDTH, PACK], BF16, name="grouped%d" % h, align_bytes=64) for h in range(HALVES)]
+        codes = [keep.tile([P, WIDTH], U32, name="codes%d" % h, align_bytes=64) for h in range(HALVES)]
+        scales = [keep.tile([P, WIDTH], U8, name="scales%d" % h, align_bytes=64) for h in range(HALVES)]
         adder = [nc.gpsimd, nc.vector]
 
         def gather(t, h):
@@ -76,56 +69,65 @@ def tile_attend_bag_bias_kernel(tc, xT, w, bias, offs, out):
         def add(t0, t1, h):
             entries = picked[h][:].rearrange("p t (g j) -> p j g t", j=BAG)
             adder[h].tensor_tensor(
-                out=e_grouped[h][:, :, t0:t1], in0=entries[:, 0, :, t0:t1], in1=entries[:, 1, :, t0:t1], op=ADD
-            )
-
-        def quantize(grouped, codes, scales):
-            nc.vector.quantize_mx(
-                out=codes[:].bitcast(FP8X4), scales=scales[:], in_=grouped[:].rearrange("p c t -> p (c t)")
+                out=grouped[h][:, M_HALF:, t0:t1], in0=entries[:, 0, :, t0:t1], in1=entries[:, 1, :, t0:t1], op=ADD
             )
 
         for t in range(PACK):
             for h in range(HALVES):
                 gather(t, h)
-            if t > 0:
-                for h in range(HALVES):
-                    add(0 if t == 1 else t, t + 1, h)
+            if t == 1:
+                add(0, 2, 0)
+                add(0, 2, 1)
+            if t == 2:
+                add(2, 3, 0)
+            if t == 3:
+                add(3, 4, 0)
+                add(2, 4, 1)
 
         for h in range(HALVES):
-            for u in range(M_HALF // P):
-                cols = slice(u * P, (u + 1) * P)
+            for u in range(TILES):
                 nc.scalar.activation(
-                    w_grouped[h][:, cols, :].rearrange("p (c i) t -> p c t i", i=4),
-                    w_raw[h][:, :, cols].rearrange("p t (c i) -> p c t i", i=4),
-                    COPY,
+                    grouped[h][:, u * P : (u + 1) * P, :].rearrange("p (c i) t -> p c t i", i=4),
+                    w_raw[h][:].rearrange("p t (c i u) -> p u c t i", i=4, u=TILES)[:, u],
+                    IDENTITY,
                 )
-        quantize(w_grouped[0], w_codes[0], w_scales[0])
         for h in range(HALVES):
-            quantize(e_grouped[h], e_codes[h], e_scales[h])
-        quantize(w_grouped[1], w_codes[1], w_scales[1])
+            nc.vector.quantize_mx(
+                out=codes[h][:].bitcast(FP8X4), scales=scales[h][:], in_=grouped[h][:].rearrange("p c t -> p (c t)")
+            )
 
-        results = [keep.tile([P, G], F32, name="result%d" % m) for m in range(M_TILES)]
-        for wh in range(HALVES):
+        result = keep.tile([P, HALVES, TILES, G], F32, name="result")
+        out_rows = out.rearrange("(h p u) g -> p h u g", h=HALVES, u=TILES)
+
+        def multiply(wh, u, h):
+            half = slice(h * G_HALF, (h + 1) * G_HALF)
+            cols = slice(u * P, (u + 1) * P)
+            acc = psum.tile([P, 512], F32, name="acc")
+            nc.tensor.matmul_mx(
+                out=acc[:, 0:G_HALF],
+                lhsT=codes[wh][:, cols].bitcast(FP8X4),
+                lhsT_scale=scales[wh][:, cols],
+                rhs=codes[h][:, M_HALF:].bitcast(FP8X4),
+                rhs_scale=scales[h][:, M_HALF:],
+                start=True,
+                stop=True,
+            )
+            dst = result[:, wh, u, half]
+            b = bias_cols[:, wh, u : u + 1]
+            if (wh, u, h) in ON_VECTOR:
+                nc.vector.tensor_scalar(dst, acc[:, 0:G_HALF], b, None, ADD)
+            else:
+                nc.scalar.activation(dst, acc[:, 0:G_HALF], IDENTITY, bias=b)
+
+        for h in range(HALVES):
+            half = slice(h * G_HALF, (h + 1) * G_HALF)
+            for u in range(TILES):
+                multiply(0, u, h)
+            nc.sync.dma_start(out_rows[:, 0, :, half], result[:, 0, :, half])
+        for u in range(TILES):
             for h in range(HALVES):
-                for u in range(M_HALF // P):
-                    m = wh * (M_HALF // P) + u
-                    cols = slice(u * P, (u + 1) * P)
-                    acc = psum.tile([P, 512], F32, name="acc")
-                    nc.tensor.matmul_mx(
-                        out=acc[:, 0:G_HALF],
-                        lhsT=w_codes[wh][:, cols].bitcast(FP8X4),
-                        lhsT_scale=w_scales[wh][:, cols],
-                        rhs=e_codes[h][:].bitcast(FP8X4),
-                        rhs_scale=e_scales[h][:],
-                        start=True,
-                        stop=True,
-                    )
-                    dst = results[m][:, h * G_HALF : (h + 1) * G_HALF]
-                    if u == 0:
-                        nc.scalar.activation(dst, acc[:, 0:G_HALF], IDENTITY, bias=bias_cols[:, m : m + 1])
-                    else:
-                        nc.vector.tensor_scalar(dst, acc[:, 0:G_HALF], bias_cols[:, m : m + 1], None, ADD)
-            for u in range(M_HALF // P):
-                m = wh * (M_HALF // P) + u
-                queue = nc.scalar if u == 0 else nc.sync
-                queue.dma_start(out[m * P : (m + 1) * P, :], results[m][:])
+                multiply(1, u, h)
+            nc.sync.dma_start(out_rows[:, 1, u, :], result[:, 1, u, :])
+
+
+ON_VECTOR = ((0, 1, 1), (1, 0, 1), (1, 1, 1))

@@ -58,31 +58,25 @@ def tile_attend_bag_bias_kernel(tc, xT, w, bias, offs, out):
         grouped = [keep.tile([P, WIDTH, PACK], BF16, name="grouped%d" % h, align_bytes=64) for h in range(HALVES)]
         codes = [keep.tile([P, WIDTH], U32, name="codes%d" % h, align_bytes=64) for h in range(HALVES)]
         scales = [keep.tile([P, WIDTH], U8, name="scales%d" % h, align_bytes=64) for h in range(HALVES)]
-        adder = [nc.gpsimd, nc.vector]
-
         def gather(t, h):
             nc.vector.tensor_copy(
                 picked[h][:, t, :],
                 planes[t][:].indirect(offsets[:, h * LIST_HALF : (h + 1) * LIST_HALF]),
             )
 
-        def add(t0, t1, h):
-            entries = picked[h][:].rearrange("p t (g j) -> p j g t", j=BAG)
-            adder[h].tensor_tensor(
-                out=grouped[h][:, M_HALF:, t0:t1], in0=entries[:, 0, :, t0:t1], in1=entries[:, 1, :, t0:t1], op=ADD
-            )
+        def add(t0, t1):
+            sums = [tile[:, M_HALF:, t0:t1] for tile in grouped]
+            pairs = picked[0][:].rearrange("p t (g j) -> p j g t", j=BAG)
+            nc.gpsimd.tensor_tensor(out=sums[0], in0=pairs[:, 0, :, t0:t1], in1=pairs[:, 1, :, t0:t1], op=ADD)
+            entries = picked[1][:].rearrange("p t (g j) -> p g t j", j=BAG)
+            with nc.allow_low_precision(reason="two float32 values are summed in float32; only the sum is rounded"):
+                nc.vector.tensor_reduce(out=sums[1], in_=entries[:, :, t0:t1, :], axis=mybir.AxisListType.X, op=ADD)
 
         for t in range(PACK):
             for h in range(HALVES):
                 gather(t, h)
-            if t == 1:
-                add(0, 2, 0)
-                add(0, 2, 1)
-            if t == 2:
-                add(2, 3, 0)
-            if t == 3:
-                add(3, 4, 0)
-                add(2, 4, 1)
+            if t > 0:
+                add(0 if t == 1 else t, t + 1)
 
         for h in range(HALVES):
             for u in range(TILES):
@@ -114,7 +108,7 @@ def tile_attend_bag_bias_kernel(tc, xT, w, bias, offs, out):
             )
             dst = result[:, wh, u, half]
             b = bias_cols[:, wh, u : u + 1]
-            if (wh, u, h) in ON_VECTOR:
+            if h == 1:
                 nc.vector.tensor_scalar(dst, acc[:, 0:G_HALF], b, None, ADD)
             else:
                 nc.scalar.activation(dst, acc[:, 0:G_HALF], IDENTITY, bias=b)
@@ -128,6 +122,3 @@ def tile_attend_bag_bias_kernel(tc, xT, w, bias, offs, out):
             for h in range(HALVES):
                 multiply(1, u, h)
             nc.sync.dma_start(out_rows[:, 1, u, :], result[:, 1, u, :])
-
-
-ON_VECTOR = ((0, 1, 1), (1, 0, 1), (1, 1, 1))

from contextlib import ExitStack

import concourse.mybir as mybir

D, T, G, BAG, M = 512, 4096, 512, 2, 512
FLOPS = 2 * D * M * G

F32 = mybir.dt.float32
BF16 = mybir.dt.bfloat16
U32 = mybir.dt.uint32
U16 = mybir.dt.uint16
U8 = mybir.dt.uint8
FP8X4 = mybir.dt.float8_e4m3fn_x4
ADD = mybir.AluOpType.add
IDENTITY = mybir.ActivationFunctionType.Identity

P = 128
PACK = 4
HALVES = 2
G_HALF = G // HALVES
E_HALF = G_HALF * BAG
LIST_HALF = E_HALF // 16
M_HALF = M // HALVES
TILES = M_HALF // P
WIDTH = M_HALF + G_HALF


def tile_attend_bag_bias_kernel(tc, xT, w, bias, offs, out):
    nc = tc.nc
    with ExitStack() as ctx:
        keep = ctx.enter_context(tc.tile_pool(name="keep", bufs=1))
        psum = ctx.enter_context(tc.psum_pool(name="psum", bufs=8))

        offsets = keep.tile([P, G * BAG // 16], U16, name="offsets")
        nc.sync.dma_start(offsets[:], offs)

        x_rows = xT.rearrange("(p t) c -> p t c", t=PACK)
        planes = []
        for t in range(PACK):
            plane = keep.tile([P, T], F32, name="plane%d" % t)
            nc.sync.dma_start(plane[:], x_rows[:, t, :])
            planes.append(plane)
        w_rows = w.rearrange("(p t) m -> p t m", t=PACK)
        w_raw = []
        for h in range(HALVES):
            raw = keep.tile([P, PACK, M_HALF], F32, name="w_raw%d" % h)
            nc.sync.dma_start(raw[:], w_rows[:, :, h * M_HALF : (h + 1) * M_HALF])
            w_raw.append(raw)
        bias_cols = keep.tile([P, HALVES, TILES], F32, name="bias_cols")
        nc.sync.dma_start(bias_cols[:], bias.rearrange("(h p u) o -> p h (u o)", h=HALVES, u=TILES))

        zero = keep.tile([P, 1], F32, name="zero")
        nc.vector.memset(zero[:], 0.0)
        loaded = keep.tile([P, 1], F32, name="loaded")
        nc.scalar.activation(loaded[:], zero[:], IDENTITY)

        picked = [keep.tile([P, PACK, E_HALF], F32, name="picked%d" % h) for h in range(HALVES)]
        grouped = [keep.tile([P, WIDTH, PACK], BF16, name="grouped%d" % h, align_bytes=64) for h in range(HALVES)]
        codes = [keep.tile([P, WIDTH], U32, name="codes%d" % h, align_bytes=64) for h in range(HALVES)]
        scales = [keep.tile([P, WIDTH], U8, name="scales%d" % h, align_bytes=64) for h in range(HALVES)]
        def gather(t, h):
            nc.vector.tensor_copy(
                picked[h][:, t, :],
                planes[t][:].indirect(offsets[:, h * LIST_HALF : (h + 1) * LIST_HALF]),
            )

        def add(t0, t1):
            sums = [tile[:, M_HALF:, t0:t1] for tile in grouped]
            pairs = picked[0][:].rearrange("p t (g j) -> p j g t", j=BAG)
            nc.gpsimd.tensor_tensor(out=sums[0], in0=pairs[:, 0, :, t0:t1], in1=pairs[:, 1, :, t0:t1], op=ADD)
            entries = picked[1][:].rearrange("p t (g j) -> p g t j", j=BAG)
            with nc.allow_low_precision(reason="two float32 values are summed in float32; only the sum is rounded"):
                nc.vector.tensor_reduce(out=sums[1], in_=entries[:, :, t0:t1, :], axis=mybir.AxisListType.X, op=ADD)

        for t in range(PACK):
            for h in range(HALVES):
                gather(t, h)
            if t > 0:
                add(0 if t == 1 else t, t + 1)

        for h in range(HALVES):
            for u in range(TILES):
                nc.scalar.activation(
                    grouped[h][:, u * P : (u + 1) * P, :].rearrange("p (c i) t -> p c t i", i=4),
                    w_raw[h][:].rearrange("p t (c i u) -> p u c t i", i=4, u=TILES)[:, u],
                    IDENTITY,
                )
        for h in range(HALVES):
            nc.vector.quantize_mx(
                out=codes[h][:].bitcast(FP8X4), scales=scales[h][:], in_=grouped[h][:].rearrange("p c t -> p (c t)")
            )

        result = keep.tile([P, HALVES, TILES, G], F32, name="result")
        out_rows = out.rearrange("(h p u) g -> p h u g", h=HALVES, u=TILES)

        def multiply(wh, u, h):
            half = slice(h * G_HALF, (h + 1) * G_HALF)
            cols = slice(u * P, (u + 1) * P)
            acc = psum.tile([P, 512], F32, name="acc")
            nc.tensor.matmul_mx(
                out=acc[:, 0:G_HALF],
                lhsT=codes[wh][:, cols].bitcast(FP8X4),
                lhsT_scale=scales[wh][:, cols],
                rhs=codes[h][:, M_HALF:].bitcast(FP8X4),
                rhs_scale=scales[h][:, M_HALF:],
                start=True,
                stop=True,
            )
            dst = result[:, wh, u, half]
            b = bias_cols[:, wh, u : u + 1]
            if h == 1:
                nc.vector.tensor_scalar(dst, acc[:, 0:G_HALF], b, None, ADD)
            else:
                nc.scalar.activation(dst, acc[:, 0:G_HALF], IDENTITY, bias=b)

        for h in range(HALVES):
            half = slice(h * G_HALF, (h + 1) * G_HALF)
            for u in range(TILES):
                multiply(0, u, h)
            nc.sync.dma_start(out_rows[:, 0, :, half], result[:, 0, :, half])
        for u in range(TILES):
            for h in range(HALVES):
                multiply(1, u, h)
            nc.sync.dma_start(out_rows[:, 1, u, :], result[:, 1, u, :])
